import numpy as np
import ml_dtypes

BF16 = ml_dtypes.bfloat16


def bf(x):
    return np.asarray(x, np.float32).astype(BF16)


def f32(x):
    return np.asarray(x, np.float32)


def f64(x):
    return np.asarray(x).astype(np.float64)


def striped(idx):
    return np.tile(idx.reshape(-1, 16).T, (8, 1))


S, K, M, N = 256, 128, 512, 64


def setup_inputs():
    return {"base": bf(np.random.standard_normal((M, S))), "x": bf(np.random.standard_normal((K, N))), "w": bf(np.random.standard_normal((K, M)) / np.sqrt(K)), "b": f32(0.5 * np.random.standard_normal((M, 1))), "offs": striped(np.random.permutation(S)[:N])}


def reference(base, x, w, b, offs):
    idx = offs[:16].T.reshape(-1)
    z = f64(base).copy()
    z[:, idx] = f64(w).T @ f64(x)
    return np.maximum(z + f64(b), 0.0)

@@ -1,0 +1,58 @@
+import concourse.mybir as mybir
+from concourse.masks import make_identity
+
+BF16, F32, U16 = mybir.dt.bfloat16, mybir.dt.float32, mybir.dt.uint16
+ADD, MAX = mybir.AluOpType.add, mybir.AluOpType.max
+RELU = mybir.ActivationFunctionType.Relu
+
+P = 128
+TOKENS = 256
+FEATURES = 512
+CONTRACTION = 128
+LISTED = 64
+GROUPS = FEATURES // P
+
+FLOPS = 2 * CONTRACTION * FEATURES * LISTED
+
+
+def tile_scatter_matmul_kernel(tc, base, x, w, b, offs, out):
+    nc = tc.nc
+    base_rows = base.rearrange("(p a) t -> p a t", a=GROUPS)
+    b_rows = b.rearrange("(p a) o -> p (a o)", a=GROUPS)
+    out_rows = out.rearrange("(p a) t -> p a t", a=GROUPS)
+
+    with (
+        tc.tile_pool(name="held", bufs=1) as held,
+        tc.psum_pool(name="psum", bufs=1) as psum,
+    ):
+        base_tile = held.tile([P, GROUPS, TOKENS], BF16)
+        w_tile = held.tile([P, FEATURES], BF16)
+        x_tile = held.tile([P, LISTED], BF16)
+        offsets = held.tile([P, LISTED // 16], U16)
+        b_tile = held.tile([P, GROUPS], F32)
+        ident = held.tile([P, P], BF16)
+
+        nc.sync.dma_start(base_tile[:], base_rows)
+        nc.sync.dma_start(w_tile[:], w)
+        nc.sync.dma_start(x_tile[:], x)
+        nc.sync.dma_start(offsets[:], offs)
+        nc.sync.dma_start(b_tile[:], b_rows)
+        make_identity(nc, ident[:])
+
+        windows = [psum.tile([P, TOKENS], F32, name=f"window{a}") for a in range(GROUPS)]
+        for a in range(GROUPS):
+            nc.tensor.matmul(windows[a][:], ident[:], base_tile[:, a, :], start=True, stop=True)
+
+        for a in range(GROUPS):
+            nc.tensor.matmul(
+                windows[a][:].indirect(offsets[:]), w_tile[:, a::GROUPS], x_tile[:], start=True, stop=True
+            )
+
+        for a in range(GROUPS):
+            result = held.tile([P, TOKENS], F32, name=f"result{a}")
+            bias = b_tile[:, a : a + 1]
+            if a % 2 == 0:
+                nc.vector.tensor_scalar(result[:], windows[a][:], bias, 0.0, ADD, MAX)
+            else:
+                nc.scalar.activation(result[:], windows[a][:], RELU, bias=bias)
+            nc.sync.dma_start(out_rows[:, a, :], result[:])

@@ -31,6 +31,8 @@ def tile_scatter_matmul_kernel(tc, base, x, w, b, offs, out):
         offsets = held.tile([P, LISTED // 16], U16)
         b_tile = held.tile([P, GROUPS], F32)
         ident = held.tile([P, P], BF16)
+        zeros = held.tile([P, 1], F32)
+        relu_of_zeros = held.tile([P, 1], F32)
 
         nc.sync.dma_start(base_tile[:], base_rows)
         nc.sync.dma_start(w_tile[:], w)
@@ -38,6 +40,8 @@ def tile_scatter_matmul_kernel(tc, base, x, w, b, offs, out):
         nc.sync.dma_start(offsets[:], offs)
         nc.sync.dma_start(b_tile[:], b_rows)
         make_identity(nc, ident[:])
+        nc.vector.memset(zeros[:], 0.0)
+        nc.scalar.activation(relu_of_zeros[:], zeros[:], RELU)
 
         windows = [psum.tile([P, TOKENS], F32, name=f"window{a}") for a in range(GROUPS)]
         for a in range(GROUPS):

@@ -11,6 +11,7 @@ FEATURES = 512
 CONTRACTION = 128
 LISTED = 64
 GROUPS = FEATURES // P
+WARM_UPS = 10
 
 FLOPS = 2 * CONTRACTION * FEATURES * LISTED
 
@@ -25,27 +26,33 @@ def tile_scatter_matmul_kernel(tc, base, x, w, b, offs, out):
         tc.tile_pool(name="held", bufs=1) as held,
         tc.psum_pool(name="psum", bufs=1) as psum,
     ):
-        base_tile = held.tile([P, GROUPS, TOKENS], BF16)
+        base_halves = [held.tile([P, GROUPS // 2, TOKENS], BF16, name=f"base_half{h}") for h in range(2)]
         w_tile = held.tile([P, FEATURES], BF16)
         x_tile = held.tile([P, LISTED], BF16)
         offsets = held.tile([P, LISTED // 16], U16)
         b_tile = held.tile([P, GROUPS], F32)
         ident = held.tile([P, P], BF16)
-        zeros = held.tile([P, 1], F32)
-        relu_of_zeros = held.tile([P, 1], F32)
+        zeros = held.tile([P, P], BF16)
+        relu_of_zeros = held.tile([P, 1], BF16)
 
-        nc.sync.dma_start(base_tile[:], base_rows)
+        for h in range(2):
+            nc.sync.dma_start(base_halves[h][:], base_rows[:, h * GROUPS // 2 : (h + 1) * GROUPS // 2, :])
         nc.sync.dma_start(w_tile[:], w)
         nc.sync.dma_start(x_tile[:], x)
         nc.sync.dma_start(offsets[:], offs)
         nc.sync.dma_start(b_tile[:], b_rows)
         make_identity(nc, ident[:])
         nc.vector.memset(zeros[:], 0.0)
-        nc.scalar.activation(relu_of_zeros[:], zeros[:], RELU)
+        nc.scalar.activation(relu_of_zeros[:], zeros[:, 0:1], RELU)
+
+        warm_bank = psum.tile([P, P], F32)
+        for turn in range(WARM_UPS):
+            nc.tensor.matmul(warm_bank[:], zeros[:], zeros[:], start=True, stop=True)
 
         windows = [psum.tile([P, TOKENS], F32, name=f"window{a}") for a in range(GROUPS)]
         for a in range(GROUPS):
-            nc.tensor.matmul(windows[a][:], ident[:], base_tile[:, a, :], start=True, stop=True)
+            half, row = divmod(a, GROUPS // 2)
+            nc.tensor.matmul(windows[a][:], ident[:], base_halves[half][:, row, :], start=True, stop=True)
 
         for a in range(GROUPS):
             nc.tensor.matmul(

import concourse.mybir as mybir
from concourse.masks import make_identity

BF16, F32, U16 = mybir.dt.bfloat16, mybir.dt.float32, mybir.dt.uint16
ADD, MAX = mybir.AluOpType.add, mybir.AluOpType.max
RELU = mybir.ActivationFunctionType.Relu

P = 128
TOKENS = 256
FEATURES = 512
CONTRACTION = 128
LISTED = 64
GROUPS = FEATURES // P
WARM_UPS = 10

FLOPS = 2 * CONTRACTION * FEATURES * LISTED


def tile_scatter_matmul_kernel(tc, base, x, w, b, offs, out):
    nc = tc.nc
    base_rows = base.rearrange("(p a) t -> p a t", a=GROUPS)
    b_rows = b.rearrange("(p a) o -> p (a o)", a=GROUPS)
    out_rows = out.rearrange("(p a) t -> p a t", a=GROUPS)

    with (
        tc.tile_pool(name="held", bufs=1) as held,
        tc.psum_pool(name="psum", bufs=1) as psum,
    ):
        base_halves = [held.tile([P, GROUPS // 2, TOKENS], BF16, name=f"base_half{h}") for h in range(2)]
        w_tile = held.tile([P, FEATURES], BF16)
        x_tile = held.tile([P, LISTED], BF16)
        offsets = held.tile([P, LISTED // 16], U16)
        b_tile = held.tile([P, GROUPS], F32)
        ident = held.tile([P, P], BF16)
        zeros = held.tile([P, P], BF16)
        relu_of_zeros = held.tile([P, 1], BF16)

        for h in range(2):
            nc.sync.dma_start(base_halves[h][:], base_rows[:, h * GROUPS // 2 : (h + 1) * GROUPS // 2, :])
        nc.sync.dma_start(w_tile[:], w)
        nc.sync.dma_start(x_tile[:], x)
        nc.sync.dma_start(offsets[:], offs)
        nc.sync.dma_start(b_tile[:], b_rows)
        make_identity(nc, ident[:])
        nc.vector.memset(zeros[:], 0.0)
        nc.scalar.activation(relu_of_zeros[:], zeros[:, 0:1], RELU)

        warm_bank = psum.tile([P, P], F32)
        for turn in range(WARM_UPS):
            nc.tensor.matmul(warm_bank[:], zeros[:], zeros[:], start=True, stop=True)

        windows = [psum.tile([P, TOKENS], F32, name=f"window{a}") for a in range(GROUPS)]
        for a in range(GROUPS):
            half, row = divmod(a, GROUPS // 2)
            nc.tensor.matmul(windows[a][:], ident[:], base_halves[half][:, row, :], start=True, stop=True)

        for a in range(GROUPS):
            nc.tensor.matmul(
                windows[a][:].indirect(offsets[:]), w_tile[:, a::GROUPS], x_tile[:], start=True, stop=True
            )

        for a in range(GROUPS):
            result = held.tile([P, TOKENS], F32, name=f"result{a}")
            bias = b_tile[:, a : a + 1]
            if a % 2 == 0:
                nc.vector.tensor_scalar(result[:], windows[a][:], bias, 0.0, ADD, MAX)
            else:
                nc.scalar.activation(result[:], windows[a][:], RELU, bias=bias)
            nc.sync.dma_start(out_rows[:, a, :], result[:])
